import numpy as np
import ml_dtypes


def mxq(x, axis, fmt="e4m3"):
    dtype, down = {"e4m3": (ml_dtypes.float8_e4m3fn, 7), "e5m2": (ml_dtypes.float8_e5m2, 14)}[fmt]
    v = np.moveaxis(np.asarray(x, np.float32).astype(ml_dtypes.bfloat16).astype(np.float64), axis, -1)
    blocks = v.reshape(v.shape[:-1] + (-1, 32))
    amax = np.abs(blocks).max(-1, keepdims=True)
    byte = np.maximum(np.where(amax > 0, np.frexp(amax)[1] - 1 + 127, 0) - down, 1)
    scale = np.exp2(byte - 127.0)
    codes = (blocks / scale).astype(np.float32).astype(dtype).astype(np.float64)
    return np.moveaxis((codes * scale).reshape(v.shape), -1, axis)


WIDE = False


def mx_kscale(k):
    if not WIDE:
        return np.ones(k)
    levels = np.array([10, -10, 5, -5, 0])
    if k % 512:
        return np.exp2(np.random.permutation(np.resize(levels, k // 32))).repeat(32)
    a = np.empty((k // 512, 16))
    for p in range(k // 512):
        a[p, :8] = np.random.permutation(np.resize(levels, 8))
        for g in range(8):
            far = levels[np.abs(levels - a[p, g]) >= 10]
            a[p, g + 8] = far[np.random.randint(len(far))]
    return np.exp2(a.ravel()).repeat(32)


def f64(x):
    return np.asarray(x).astype(np.float64)


def striped(idx):
    return np.tile(idx.reshape(-1, 16).T, (8, 1)).astype(np.uint16)


def unstriped(offs):
    return offs[:16].T.reshape(-1).astype(np.int64)


E2M1 = np.array([0.0, 0.5, 1.0, 1.5, 2.0, 3.0, 4.0, 6.0, -0.0, -0.5, -1.0, -1.5, -2.0, -3.0, -4.0, -6.0])


def pack_weight(w, fmt):
    k, n = w.shape
    w = f64(np.asarray(w, np.float32).astype(ml_dtypes.bfloat16)).reshape(k // 32, 32, n)
    amax = np.abs(w).max(1)
    if fmt == "e4m3":
        byte = np.frexp(amax)[1] - 1 + 127 - 7
    else:
        mant, ex = np.frexp(amax / 6.0)
        byte = np.where(mant > 0.5, ex, ex - 1) + 127
    byte = np.clip(np.where(amax > 0, byte, 1), 1, 254)
    scaled = (w * np.exp2(127.0 - byte)[:, None, :]).reshape(k, n).astype(np.float32)
    by_word = np.ascontiguousarray(scaled.reshape(k // 512, 128, 4, n).transpose(0, 1, 3, 2))
    if fmt == "e4m3":
        words = by_word.astype(ml_dtypes.float8_e4m3fn).view(np.uint8)
    else:
        c = by_word.astype(ml_dtypes.float4_e2m1fn).view(np.uint8) & 0xF
        words = (c[..., 0::2] | (c[..., 1::2] << 4)).reshape(k // 512, 128, 2 * n)
    return np.ascontiguousarray(words), np.ascontiguousarray(byte.astype(np.uint8).reshape(k // 512, 16, n))


def unpack_weight(words, scales, fmt):
    g, _, n = scales.shape
    words = np.ascontiguousarray(words).reshape(g, 128, n, -1)
    if fmt == "e4m3":
        vals = words.view(ml_dtypes.float8_e4m3fn).astype(np.float64)
    else:
        nib = np.empty((g, 128, n, 4), np.uint8)
        nib[..., 0::2] = words & 0xF
        nib[..., 1::2] = words >> 4
        vals = E2M1[nib]
    vals = vals * np.repeat(np.exp2(scales.astype(np.float64) - 127.0), 8, axis=1)[..., None]
    return vals.transpose(0, 1, 3, 2).reshape(g * 512, n)


def gelu(v):
    return 0.5 * v * (1.0 + np.tanh(np.sqrt(2.0 / np.pi) * (v + 0.044715 * v**3)))


K, L, H, N, T, S = 1024, 512, 1024, 512, 2048, 1024

def setup_inputs():
    n = np.random.standard_normal
    s = mx_kscale(K)[:, None]
    s2 = mx_kscale(L)[:, None]
    u = mx_kscale(H)[:, None]
    tab_words, tab_scales = pack_weight(n((K, T)) * s, "e4m3")
    tab2_words, tab2_scales = pack_weight(n((L, T)) * s2, "e4m3")
    b4_words, b4_scales = pack_weight(n((L, H)) / np.sqrt(L) / s2 * u.T, "e2m1")
    return {
        "tab_words": tab_words, "tab_scales": tab_scales,
        "tab2_words": tab2_words, "tab2_scales": tab2_scales,
        "offs": striped(np.random.permutation(T)[:S]),
        "offs2": striped(np.random.permutation(T)[:S]),
        "a": (n((K, H)) / np.sqrt(K) / s * u.T).astype(np.float32),
        "b4_words": b4_words, "b4_scales": b4_scales,
        "gT": ((0.3 + 0.2 * n((H, T))) * u).astype(np.float32),
        "w": (n((H, N)) / np.sqrt(H) / u).astype(np.float32),
        "bias": (0.3 * n(N)).astype(np.float32),
    }

def reference(tab_words, tab_scales, tab2_words, tab2_scales, offs, offs2, a, b4_words, b4_scales, gT, w, bias):
    v = unpack_weight(tab_words, tab_scales, "e4m3")[:, unstriped(offs)]
    v2 = unpack_weight(tab2_words, tab2_scales, "e4m3")[:, unstriped(offs2)]
    g = f64(gT)[:, unstriped(offs)]
    p = mxq(f64(a), 0, "e4m3").T @ v
    q = unpack_weight(b4_words, b4_scales, "e2m1").T @ v2
    h = np.maximum(np.maximum(p, q) - g, 0.0)
    y = mxq(f64(w), 0, "e4m3").T @ mxq(h, 0, "e4m3")
    return y + f64(bias)[:, None]

@@ -1,0 +1,271 @@
+from contextlib import ExitStack
+
+import concourse.mybir as mybir
+
+K, L, H, N, T, S = 1024, 512, 1024, 512, 2048, 1024
+FLOPS = 2 * S * (K * H + L * H + H * N)
+
+F32 = mybir.dt.float32
+BF16 = mybir.dt.bfloat16
+I32 = mybir.dt.int32
+U32 = mybir.dt.uint32
+U16 = mybir.dt.uint16
+U8 = mybir.dt.uint8
+FP8X4 = mybir.dt.float8_e4m3fn_x4
+FP4X4 = mybir.dt.float4_e2m1fn_x4
+ALU = mybir.AluOpType
+ACT = mybir.ActivationFunctionType
+
+P = 128
+PACK = 4
+PASS = P * PACK
+HALF = 512
+LANES = 16
+CHUNKS = [(0, 512), (512, 256), (768, 256)]
+
+
+def tile_list_residue_contact_max_kernel(
+    tc, tab_words, tab_scales, tab2_words, tab2_scales, offs, offs2, a, b4_words, b4_scales, gT, w, bias, out
+):
+    nc = tc.nc
+    with ExitStack() as ctx:
+        keep = ctx.enter_context(tc.tile_pool(name="keep", bufs=1))
+        ring = ctx.enter_context(tc.tile_pool(name="ring", bufs=1))
+        psum = ctx.enter_context(tc.psum_pool(name="psum", bufs=1))
+
+        idx2 = keep.tile([P, S // LANES], U16, name="idx2")
+        nc.sync.dma_start(idx2[:], offs2)
+        idx = keep.tile([P, S // LANES], U16, name="idx")
+        nc.sync.dma_start(idx[:], offs)
+
+        def load_scale_rows(scales, name):
+            passes, width = scales.shape[0], scales.shape[2]
+            plane = keep.tile([P, width], U8, name=name, align_bytes=64)
+            nc.vector.memset(plane[:].bitcast(I32), 0)
+            for quad in range(4):
+                rows = scales[:, 4 * quad : 4 * quad + 4, :] if passes > 1 else scales[0, 4 * quad : 4 * quad + 4, :]
+                nc.sync.dma_start(plane[32 * quad : 32 * quad + 4 * passes, :].bitcast(I32), rows.bitcast(I32))
+            return plane
+
+        def load_words(words, name):
+            table = keep.tile([P, T], I32, name=name, align_bytes=64)
+            nc.sync.dma_start(table[:], words.rearrange("p n i -> p (n i)").bitcast(I32))
+            return table
+
+        def load_weight(rows):
+            raw = ring.tile([P, PACK, PASS], F32, name="raw", tag="raw", bufs=5)
+            nc.sync.dma_start(raw[:], rows.rearrange("(p i) c -> p i c", i=PACK))
+            return raw
+
+        def load_thresholds(blk, t):
+            rows = keep.tile([P, T], F32, name="g%d%d" % (blk, t), align_bytes=64)
+            nc.sync.dma_start(rows[:], gT[blk * PASS : (blk + 1) * PASS, :].rearrange("(p t) c -> p t c", t=PACK)[:, t, :])
+            return rows
+
+        tab2_plane = load_scale_rows(tab2_scales, "tab2_plane")
+        tab2_table = load_words(tab2_words[0], "tab2_table")
+        b4_raw = keep.tile([P, 2 * H], U8, name="b4_raw", align_bytes=64)
+        nc.sync.dma_start(b4_raw[:].bitcast(I32), b4_words[0].bitcast(I32))
+        a_raw, w_raw, g_rows = {}, {}, {}
+        a_raw[0, 0] = load_weight(a[0:PASS, 0:PASS])
+        tab_plane = load_scale_rows(tab_scales, "tab_plane")
+        tab_table0 = load_words(tab_words[0], "tab_table0")
+        b4_plane = load_scale_rows(b4_scales, "b4_plane")
+        a_raw[1, 0] = load_weight(a[PASS:K, 0:PASS])
+        tab_table1 = load_words(tab_words[1], "tab_table1")
+        for t in range(PACK):
+            g_rows[0, t] = load_thresholds(0, t)
+        a_raw[0, 1] = load_weight(a[0:PASS, PASS:H])
+        for t in range(PACK - 1):
+            g_rows[1, t] = load_thresholds(1, t)
+        a_raw[1, 1] = load_weight(a[PASS:K, PASS:H])
+        g_rows[1, 3] = load_thresholds(1, 3)
+        w_raw[0] = load_weight(w[0:PASS, :])
+        w_raw[1] = load_weight(w[PASS:H, :])
+        bias_cols = keep.tile([P, PACK], F32, name="bias_cols")
+        nc.sync.dma_start(bias_cols[:], bias.rearrange("(p t) -> p t", t=PACK))
+
+        def offsets(lst, first, count):
+            return lst[:, first // LANES : (first + count) // LANES]
+
+        def pick(window, lst, half, dtype, name):
+            picked = keep.tile([P, HALF], dtype, name="%s_%d" % (name, half), align_bytes=64)
+            nc.vector.tensor_copy(picked[:], window.indirect(offsets(lst, half * HALF, HALF)))
+            return picked
+
+        def round_weight(raw):
+            grouped = ring.tile([P, PACK * PASS], BF16, name="grouped", tag="grouped", bufs=4, align_bytes=64)
+            nc.scalar.copy(
+                out=grouped[:].rearrange("p (t m i) -> p m i t", t=PACK, i=PACK),
+                in_=raw[:].rearrange("p i (m t) -> p m i t", t=PACK),
+            )
+            return grouped
+
+        def quantise(grouped, name):
+            width = grouped.shape[1] // PACK
+            codes = keep.tile([P, width], U32, name=name + "_codes", align_bytes=64)
+            scales = keep.tile([P, width], U8, name=name + "_scales", align_bytes=64)
+            nc.vector.quantize_mx(out=codes[:].bitcast(FP8X4), scales=scales[:], in_=grouped[:])
+            return codes, scales
+
+        v2_scales = [pick(tab2_plane[:], idx2, h, U8, "v2_scales") for h in range(2)]
+        v2_words = [pick(tab2_table[:].bitcast(U32), idx2, h, U32, "v2_words") for h in range(2)]
+        a_mx, w_mx, h_mx = {}, {}, {}
+        grouped_a00 = round_weight(a_raw[0, 0])
+        grouped_a10 = round_weight(a_raw[1, 0])
+        v_scales = [pick(tab_plane[:], idx, h, U8, "v_scales") for h in range(2)]
+        v_words = {(0, h): pick(tab_table0[:].bitcast(U32), idx, h, U32, "v_words0") for h in range(2)}
+
+        b4_codes = keep.tile([P, 2 * H], U8, name="b4_codes", align_bytes=64)
+        nc.vector.tensor_copy(
+            out=b4_codes[:].bitcast(U16).rearrange("p (b t m) -> p b t m", t=PACK, m=P),
+            in_=b4_raw[:].bitcast(U16).rearrange("p (b m t) -> p b t m", t=PACK, m=P),
+        )
+        b4_dealt = keep.tile([P, H], U8, name="b4_dealt", align_bytes=64)
+        nc.vector.tensor_copy(
+            out=b4_dealt[:].rearrange("p (b t m) -> p b t m", t=PACK, m=P),
+            in_=b4_plane[:].rearrange("p (b m t) -> p b t m", t=PACK, m=P),
+        )
+        a_mx[0, 0] = quantise(grouped_a00, "a00")
+        v_words[1, 0] = pick(tab_table1[:].bitcast(U32), idx, 0, U32, "v_words1")
+        a_mx[1, 0] = quantise(grouped_a10, "a10")
+        v_words[1, 1] = pick(tab_table1[:].bitcast(U32), idx, 1, U32, "v_words1")
+
+        def larger_projection(blk, t, half):
+            cols = slice(t * P, (t + 1) * P)
+            first = blk * PASS + t * P
+            q_acc = psum.tile([P, HALF], F32, name="q_acc", tag="q", bufs=2)
+            nc.tensor.matmul_mx(
+                q_acc[:],
+                lhsT=b4_codes[:, 2 * first : 2 * (first + P)].bitcast(FP4X4),
+                lhsT_scale=b4_dealt[:, first : first + P],
+                rhs=v2_words[half][:].bitcast(FP8X4),
+                rhs_scale=v2_scales[half][:],
+                start=True,
+                stop=True,
+            )
+            q_rows = ring.tile([P, HALF], F32, name="q_rows", tag="q_rows", bufs=4)
+            nc.scalar.copy(out=q_rows[:], in_=q_acc[:])
+            p_acc = psum.tile([P, HALF], F32, name="p_acc", tag="p", bufs=3)
+            for c in range(2):
+                codes, scales = a_mx[c, blk]
+                nc.tensor.matmul_mx(
+                    p_acc[:],
+                    lhsT=codes[:, cols].bitcast(FP8X4),
+                    lhsT_scale=scales[:, cols],
+                    rhs=v_words[c, half][:].bitcast(FP8X4),
+                    rhs_scale=v_scales[half][4 * c : P, :],
+                    start=(c == 0),
+                    stop=(c == 1),
+                )
+            larger = ring.tile([P, HALF], F32, name="larger", tag="larger", bufs=5)
+            nc.vector.tensor_tensor(larger[:], p_acc[:], q_rows[:], ALU.max)
+            return larger
+
+        def shortfall(short, larger, blk, t, first, count):
+            lo = first % HALF
+            nc.vector.tensor_tensor(
+                short[:, t, lo : lo + count],
+                g_rows[blk, t][:].indirect(offsets(idx, first, count)),
+                larger[:, lo : lo + count],
+                ALU.subtract,
+            )
+
+        def clamp(short, first, count):
+            lo = first % HALF
+            grouped = ring.tile([P, PACK * count], BF16, name="grouped", tag="grouped", bufs=4, align_bytes=64)
+            nc.scalar.activation(
+                out=grouped[:].rearrange("p (c i t) -> p c t i", t=PACK, i=4),
+                in_=short[:, :, lo : lo + count].rearrange("p t (c i) -> p c t i", i=4),
+                func=ACT.Relu,
+                scale=-1.0,
+            )
+            return grouped
+
+        out_rows = out.rearrange("(p t) j -> p t j", t=PACK)
+
+        def features(first, count, last):
+            half, lo = divmod(first, HALF)
+            staged = ring.tile([P, PACK, count], F32, name="staged", tag="raw", bufs=5)
+            for t in range(PACK):
+                cols = slice(t * P, (t + 1) * P)
+                tag, bufs = (("p", 3), ("q", 2))[t // 2] if last else ("y", 3)
+                y_acc = psum.tile([P, count], F32, name="y_acc", tag=tag, bufs=bufs)
+                operands = [(h_mx[0, half], slice(lo, lo + count)), (h_mx[1, first], slice(0, count))]
+                for blk, ((codes, scales), span) in enumerate(operands):
+                    nc.tensor.matmul_mx(
+                        y_acc[:],
+                        lhsT=w_mx[blk][0][:, cols].bitcast(FP8X4),
+                        lhsT_scale=w_mx[blk][1][:, cols],
+                        rhs=codes[:, span].bitcast(FP8X4),
+                        rhs_scale=scales[:, span],
+                        start=(blk == 0),
+                        stop=(blk == 1),
+                    )
+                if last and t % 2 == 0:
+                    nc.vector.tensor_scalar(staged[:, t, :], y_acc[:], bias_cols[:, t : t + 1], None, ALU.add)
+                else:
+                    nc.scalar.activation(out=staged[:, t, :], in_=y_acc[:], func=ACT.Identity, bias=bias_cols[:, t : t + 1])
+            nc.sync.dma_start(out_rows[:, :, first : first + count], staged[:])
+
+        def new_short():
+            return ring.tile([P, PACK, HALF], F32, name="short", tag="short", bufs=3)
+
+        short0 = [new_short() for h in range(2)]
+        units = [(t, h) for t in range(PACK) for h in range(2)]
+        pending = None
+        grouped_a = {}
+        for t, h in units:
+            larger = larger_projection(0, t, h)
+            if pending:
+                shortfall(*pending)
+            pending = (short0[h], larger, 0, t, h * HALF, HALF)
+            if (t, h) == (2, 0):
+                grouped_a[0] = round_weight(a_raw[0, 1])
+            if (t, h) == (3, 0):
+                a_mx[0, 1] = quantise(grouped_a[0], "a01")
+                grouped_a[1] = round_weight(a_raw[1, 1])
+            if (t, h) == (3, 1):
+                a_mx[1, 1] = quantise(grouped_a[1], "a11")
+                grouped_h00 = clamp(short0[0], 0, HALF)
+
+        short1 = new_short()
+        for t in range(PACK):
+            larger = larger_projection(1, t, 0)
+            shortfall(*pending)
+            pending = (short1, larger, 1, t, 0, HALF)
+            if t == 0:
+                grouped_h01 = clamp(short0[1], HALF, HALF)
+            if t == 1:
+                h_mx[0, 0] = quantise(grouped_h00, "h00")
+                grouped_w0 = round_weight(w_raw[0])
+            if t == 2:
+                h_mx[0, 1] = quantise(grouped_h01, "h01")
+            if t == 3:
+                w_mx[0] = quantise(grouped_w0, "w0")
+                grouped_w1 = round_weight(w_raw[1])
+
+        short2 = new_short()
+        kept = []
+        for t in range(PACK):
+            larger = larger_projection(1, t, 1)
+            kept.append(larger)
+            shortfall(*pending)
+            pending = (short2, larger, 1, t) + CHUNKS[1]
+            if t == 0:
+                grouped_h10 = clamp(short1, 0, HALF)
+            if t == 2:
+                w_mx[1] = quantise(grouped_w1, "w1")
+            if t == 3:
+                h_mx[1, 0] = quantise(grouped_h10, "h10")
+                features(0, HALF, False)
+        shortfall(*pending)
+        grouped_b = clamp(short2, *CHUNKS[1])
+        for t in range(PACK):
+            shortfall(short2, kept[t], 1, t, *CHUNKS[2])
+            if t == 2:
+                h_mx[1, CHUNKS[1][0]] = quantise(grouped_b, "h11")
+                features(CHUNKS[1][0], CHUNKS[1][1], False)
+        grouped_c = clamp(short2, *CHUNKS[2])
+        h_mx[1, CHUNKS[2][0]] = quantise(grouped_c, "h12")
+        features(CHUNKS[2][0], CHUNKS[2][1], True)

@@ -21,7 +21,10 @@ PACK = 4
 PASS = P * PACK
 HALF = 512
 LANES = 16
-CHUNKS = [(0, 512), (512, 256), (768, 256)]
+RAW_BUFS = 5
+GROUPED_BUFS = 6
+LARGER_BUFS = 3
+CHUNKS = [(512, 128), (640, 128), (768, 128), (896, 128)]
 
 
 def tile_list_residue_contact_max_kernel(
@@ -33,11 +36,6 @@ def tile_list_residue_contact_max_kernel(
         ring = ctx.enter_context(tc.tile_pool(name="ring", bufs=1))
         psum = ctx.enter_context(tc.psum_pool(name="psum", bufs=1))
 
-        idx2 = keep.tile([P, S // LANES], U16, name="idx2")
-        nc.sync.dma_start(idx2[:], offs2)
-        idx = keep.tile([P, S // LANES], U16, name="idx")
-        nc.sync.dma_start(idx[:], offs)
-
         def load_scale_rows(scales, name):
             passes, width = scales.shape[0], scales.shape[2]
             plane = keep.tile([P, width], U8, name=name, align_bytes=64)
@@ -48,40 +46,46 @@ def tile_list_residue_contact_max_kernel(
             return plane
 
         def load_words(words, name):
-            table = keep.tile([P, T], I32, name=name, align_bytes=64)
+            table = ring.tile([P, T], I32, name=name, tag=name, align_bytes=64)
             nc.sync.dma_start(table[:], words.rearrange("p n i -> p (n i)").bitcast(I32))
             return table
 
-        def load_weight(rows):
-            raw = ring.tile([P, PACK, PASS], F32, name="raw", tag="raw", bufs=5)
+        def load_weight(rows, tag="raw", bufs=RAW_BUFS):
+            raw = ring.tile([P, PACK, PASS], F32, name="raw", tag=tag, bufs=bufs, align_bytes=64)
             nc.sync.dma_start(raw[:], rows.rearrange("(p i) c -> p i c", i=PACK))
             return raw
 
         def load_thresholds(blk, t):
-            rows = keep.tile([P, T], F32, name="g%d%d" % (blk, t), align_bytes=64)
+            name = "g%d%d" % (blk, t)
+            rows = ring.tile([P, T], F32, name=name, tag=name, align_bytes=64)
             nc.sync.dma_start(rows[:], gT[blk * PASS : (blk + 1) * PASS, :].rearrange("(p t) c -> p t c", t=PACK)[:, t, :])
             return rows
 
-        tab2_plane = load_scale_rows(tab2_scales, "tab2_plane")
+        a_raw, w_raw, g_rows = {}, {}, {}
         tab2_table = load_words(tab2_words[0], "tab2_table")
+        idx2 = keep.tile([P, S // LANES], U16, name="idx2")
+        nc.sync.dma_start(idx2[:], offs2)
+        tab2_plane = load_scale_rows(tab2_scales, "tab2_plane")
+        a_raw[0, 0] = load_weight(a[0:PASS, 0:PASS])
+        idx = keep.tile([P, S // LANES], U16, name="idx")
+        nc.sync.dma_start(idx[:], offs)
+        tab_plane = load_scale_rows(tab_scales, "tab_plane")
         b4_raw = keep.tile([P, 2 * H], U8, name="b4_raw", align_bytes=64)
         nc.sync.dma_start(b4_raw[:].bitcast(I32), b4_words[0].bitcast(I32))
-        a_raw, w_raw, g_rows = {}, {}, {}
-        a_raw[0, 0] = load_weight(a[0:PASS, 0:PASS])
-        tab_plane = load_scale_rows(tab_scales, "tab_plane")
-        tab_table0 = load_words(tab_words[0], "tab_table0")
         b4_plane = load_scale_rows(b4_scales, "b4_plane")
-        a_raw[1, 0] = load_weight(a[PASS:K, 0:PASS])
+        tab_table0 = load_words(tab_words[0], "tab_table0")
+        a_raw[1, 0] = load_weight(a[PASS:K, 0:PASS], "a10_raw", 1)
         tab_table1 = load_words(tab_words[1], "tab_table1")
-        for t in range(PACK):
-            g_rows[0, t] = load_thresholds(0, t)
+        g_rows[0, 0] = load_thresholds(0, 0)
         a_raw[0, 1] = load_weight(a[0:PASS, PASS:H])
-        for t in range(PACK - 1):
-            g_rows[1, t] = load_thresholds(1, t)
+        g_rows[0, 1] = load_thresholds(0, 1)
         a_raw[1, 1] = load_weight(a[PASS:K, PASS:H])
-        g_rows[1, 3] = load_thresholds(1, 3)
+        g_rows[0, 2] = load_thresholds(0, 2)
         w_raw[0] = load_weight(w[0:PASS, :])
+        g_rows[0, 3] = load_thresholds(0, 3)
         w_raw[1] = load_weight(w[PASS:H, :])
+        for t in range(PACK):
+            g_rows[1, t] = load_thresholds(1, t)
         bias_cols = keep.tile([P, PACK], F32, name="bias_cols")
         nc.sync.dma_start(bias_cols[:], bias.rearrange("(p t) -> p t", t=PACK))
 
@@ -93,20 +97,30 @@ def tile_list_residue_contact_max_kernel(
             nc.vector.tensor_copy(picked[:], window.indirect(offsets(lst, half * HALF, HALF)))
             return picked
 
-        def round_weight(raw):
-            grouped = ring.tile([P, PACK * PASS], BF16, name="grouped", tag="grouped", bufs=4, align_bytes=64)
+        def round_weight(raw, tag="grouped", bufs=GROUPED_BUFS):
+            grouped = ring.tile([P, PACK * PASS], BF16, name="grouped", tag=tag, bufs=bufs, align_bytes=64)
             nc.scalar.copy(
                 out=grouped[:].rearrange("p (t m i) -> p m i t", t=PACK, i=PACK),
                 in_=raw[:].rearrange("p i (m t) -> p m i t", t=PACK),
             )
             return grouped
 
-        def quantise(grouped, name):
+        def quantise(grouped, name, codes=None, scales=None):
             width = grouped.shape[1] // PACK
-            codes = keep.tile([P, width], U32, name=name + "_codes", align_bytes=64)
-            scales = keep.tile([P, width], U8, name=name + "_scales", align_bytes=64)
-            nc.vector.quantize_mx(out=codes[:].bitcast(FP8X4), scales=scales[:], in_=grouped[:])
+            if codes is None:
+                codes = keep.tile([P, width], U32, name=name + "_codes", align_bytes=64)[:]
+            if scales is None:
+                scales = keep.tile([P, width], U8, name=name + "_scales", align_bytes=64)[:]
+            nc.vector.quantize_mx(out=codes.bitcast(FP8X4), scales=scales, in_=grouped[:])
             return codes, scales
+
+        def held_scales(name, count):
+            planes = ring.tile([P, count * PASS], U8, name=name, tag="larger", bufs=LARGER_BUFS, align_bytes=64)
+            return [planes[:, n * PASS : (n + 1) * PASS] for n in range(count)]
+
+        def codes_pair(name, tag):
+            pair = ring.tile([P, 2 * PASS], U32, name=name, tag=tag, align_bytes=64)
+            return pair[:, 0:PASS], pair[:, PASS : 2 * PASS]
 
         v2_scales = [pick(tab2_plane[:], idx2, h, U8, "v2_scales") for h in range(2)]
         v2_words = [pick(tab2_table[:].bitcast(U32), idx2, h, U32, "v2_words") for h in range(2)]
@@ -115,6 +129,8 @@ def tile_list_residue_contact_max_kernel(
         grouped_a10 = round_weight(a_raw[1, 0])
         v_scales = [pick(tab_plane[:], idx, h, U8, "v_scales") for h in range(2)]
         v_words = {(0, h): pick(tab_table0[:].bitcast(U32), idx, h, U32, "v_words0") for h in range(2)}
+        first_codes = codes_pair("a0_codes", "tab_table0")
+        a_mx[0, 0] = quantise(grouped_a00, "a00", first_codes[0])
 
         b4_codes = keep.tile([P, 2 * H], U8, name="b4_codes", align_bytes=64)
         nc.vector.tensor_copy(
@@ -126,26 +142,29 @@ def tile_list_residue_contact_max_kernel(
             out=b4_dealt[:].rearrange("p (b t m) -> p b t m", t=PACK, m=P),
             in_=b4_plane[:].rearrange("p (b m t) -> p b t m", t=PACK, m=P),
         )
-        a_mx[0, 0] = quantise(grouped_a00, "a00")
+        a_mx[1, 0] = quantise(grouped_a10, "a10", first_codes[1])
         v_words[1, 0] = pick(tab_table1[:].bitcast(U32), idx, 0, U32, "v_words1")
-        a_mx[1, 0] = quantise(grouped_a10, "a10")
         v_words[1, 1] = pick(tab_table1[:].bitcast(U32), idx, 1, U32, "v_words1")
 
-        def larger_projection(blk, t, half):
+        def contact_projections(units, tag):
+            q_rows = ring.tile([P, len(units) * HALF], F32, name="q_rows", tag=tag, align_bytes=64)
+            for n, (blk, t, half) in enumerate(units):
+                first = blk * PASS + t * P
+                q_acc = psum.tile([P, HALF], F32, name="q_acc", tag="q", bufs=2)
+                nc.tensor.matmul_mx(
+                    q_acc[:],
+                    lhsT=b4_codes[:, 2 * first : 2 * (first + P)].bitcast(FP4X4),
+                    lhsT_scale=b4_dealt[:, first : first + P],
+                    rhs=v2_words[half][:].bitcast(FP8X4),
+                    rhs_scale=v2_scales[half][:],
+                    start=True,
+                    stop=True,
+                )
+                nc.scalar.copy(out=q_rows[:, n * HALF : (n + 1) * HALF], in_=q_acc[:])
+                q_of[blk, t, half] = q_rows[:, n * HALF : (n + 1) * HALF]
+
+        def larger_projection(blk, t, half, larger):
             cols = slice(t * P, (t + 1) * P)
-            first = blk * PASS + t * P
-            q_acc = psum.tile([P, HALF], F32, name="q_acc", tag="q", bufs=2)
-            nc.tensor.matmul_mx(
-                q_acc[:],
-                lhsT=b4_codes[:, 2 * first : 2 * (first + P)].bitcast(FP4X4),
-                lhsT_scale=b4_dealt[:, first : first + P],
-                rhs=v2_words[half][:].bitcast(FP8X4),
-                rhs_scale=v2_scales[half][:],
-                start=True,
-                stop=True,
-            )
-            q_rows = ring.tile([P, HALF], F32, name="q_rows", tag="q_rows", bufs=4)
-            nc.scalar.copy(out=q_rows[:], in_=q_acc[:])
             p_acc = psum.tile([P, HALF], F32, name="p_acc", tag="p", bufs=3)
             for c in range(2):
                 codes, scales = a_mx[c, blk]
@@ -158,114 +177,165 @@ def tile_list_residue_contact_max_kernel(
                     start=(c == 0),
                     stop=(c == 1),
                 )
-            larger = ring.tile([P, HALF], F32, name="larger", tag="larger", bufs=5)
-            nc.vector.tensor_tensor(larger[:], p_acc[:], q_rows[:], ALU.max)
-            return larger
+            nc.vector.tensor_tensor(larger, p_acc[:], q_of[blk, t, half], ALU.max)
+
+        def new_larger(tag="larger", bufs=LARGER_BUFS):
+            larger = ring.tile([P, HALF], F32, name="larger", tag=tag, bufs=bufs, align_bytes=64)
+            return larger[:]
+
+        def new_short(count):
+            return ring.tile([P, PACK, count], F32, name="short", tag="short", bufs=3)
 
         def shortfall(short, larger, blk, t, first, count):
             lo = first % HALF
             nc.vector.tensor_tensor(
-                short[:, t, lo : lo + count],
+                short[:, t % short.shape[1], :],
                 g_rows[blk, t][:].indirect(offsets(idx, first, count)),
                 larger[:, lo : lo + count],
                 ALU.subtract,
             )
 
-        def clamp(short, first, count):
-            lo = first % HALF
-            grouped = ring.tile([P, PACK * count], BF16, name="grouped", tag="grouped", bufs=4, align_bytes=64)
-            nc.scalar.activation(
-                out=grouped[:].rearrange("p (c i t) -> p c t i", t=PACK, i=4),
-                in_=short[:, :, lo : lo + count].rearrange("p t (c i) -> p c t i", i=4),
-                func=ACT.Relu,
-                scale=-1.0,
-            )
+        def clamp(short, tag="grouped", bufs=GROUPED_BUFS):
+            count = short.shape[2]
+            grouped = ring.tile([P, PACK * count], BF16, name="grouped", tag=tag, bufs=bufs, align_bytes=64)
+            woven = grouped[:].rearrange("p (c i t) -> p c t i", t=PACK, i=4)
+            slices = short[:].rearrange("p t (c i) -> p c t i", i=4)
+            nc.scalar.activation(out=woven, in_=slices, func=ACT.Relu, scale=-1.0)
             return grouped
 
         out_rows = out.rearrange("(p t) j -> p t j", t=PACK)
 
-        def features(first, count, last):
+        def feature_sums(y_acc, t, first, count):
             half, lo = divmod(first, HALF)
-            staged = ring.tile([P, PACK, count], F32, name="staged", tag="raw", bufs=5)
+            cols = slice(t * P, (t + 1) * P)
+            operands = [(h_mx[0, half], slice(lo, lo + count)), (h_mx[1, first], slice(0, count))]
+            for blk, ((codes, scales), span) in enumerate(operands):
+                nc.tensor.matmul_mx(
+                    y_acc,
+                    lhsT=w_mx[blk][0][:, cols].bitcast(FP8X4),
+                    lhsT_scale=w_mx[blk][1][:, cols],
+                    rhs=codes[:, span].bitcast(FP8X4),
+                    rhs_scale=scales[:, span],
+                    start=(blk == 0),
+                    stop=(blk == 1),
+                )
+
+        def add_bias(staged, y_acc, t, on_vector=False):
+            if on_vector:
+                nc.vector.tensor_scalar(staged[:, t, :], y_acc, bias_cols[:, t : t + 1], None, ALU.add)
+            else:
+                nc.scalar.activation(out=staged[:, t, :], in_=y_acc, func=ACT.Identity, bias=bias_cols[:, t : t + 1])
+
+        def new_staged(count):
+            return ring.tile([P, PACK, count], F32, name="staged", tag="raw", bufs=RAW_BUFS, align_bytes=64)
+
+        def features_of_half():
+            staged = new_staged(HALF)
             for t in range(PACK):
-                cols = slice(t * P, (t + 1) * P)
-                tag, bufs = (("p", 3), ("q", 2))[t // 2] if last else ("y", 3)
-                y_acc = psum.tile([P, count], F32, name="y_acc", tag=tag, bufs=bufs)
-                operands = [(h_mx[0, half], slice(lo, lo + count)), (h_mx[1, first], slice(0, count))]
-                for blk, ((codes, scales), span) in enumerate(operands):
-                    nc.tensor.matmul_mx(
-                        y_acc[:],
-                        lhsT=w_mx[blk][0][:, cols].bitcast(FP8X4),
-                        lhsT_scale=w_mx[blk][1][:, cols],
-                        rhs=codes[:, span].bitcast(FP8X4),
-                        rhs_scale=scales[:, span],
-                        start=(blk == 0),
-                        stop=(blk == 1),
-                    )
-                if last and t % 2 == 0:
-                    nc.vector.tensor_scalar(staged[:, t, :], y_acc[:], bias_cols[:, t : t + 1], None, ALU.add)
-                else:
-                    nc.scalar.activation(out=staged[:, t, :], in_=y_acc[:], func=ACT.Identity, bias=bias_cols[:, t : t + 1])
+                y_acc = psum.tile([P, HALF], F32, name="y_acc", tag="y", bufs=3)
+                feature_sums(y_acc[:], t, 0, HALF)
+                add_bias(staged, y_acc[:], t)
+                nc.sync.dma_start(out_rows[:, t, 0:HALF], staged[:, t, :])
+
+        def features_of_chunk(first, count):
+            staged = new_staged(count)
+            y_acc = psum.tile([P, PACK, count], F32, name="y_acc", tag="y", bufs=3)
+            for t in range(PACK):
+                feature_sums(y_acc[:, t, :], t, first, count)
+            for t in range(PACK):
+                add_bias(staged, y_acc[:, t, :], t)
             nc.sync.dma_start(out_rows[:, :, first : first + count], staged[:])
 
-        def new_short():
-            return ring.tile([P, PACK, HALF], F32, name="short", tag="short", bufs=3)
+        def features_of_last_chunk(first, count):
+            staged = new_staged(count)
+            for t in range(PACK):
+                tag, bufs = (("p", 3), ("q", 2))[t // 2]
+                y_acc = psum.tile([P, count], F32, name="y_acc", tag=tag, bufs=bufs)
+                feature_sums(y_acc[:], t, first, count)
+                add_bias(staged, y_acc[:], t, on_vector=t % 2 == 0)
+            nc.sync.dma_start(out_rows[:, :, first : first + count], staged[:])
 
-        short0 = [new_short() for h in range(2)]
-        units = [(t, h) for t in range(PACK) for h in range(2)]
+        q_of = {}
+        units0 = [(0, t, h) for t in range(PACK) for h in range(2)]
+        contact_projections(units0[:4], "a10_raw")
+        contact_projections(units0[4:], "tab_table1")
+
+        short0 = [new_short(HALF) for h in range(2)]
         pending = None
-        grouped_a = {}
-        for t, h in units:
-            larger = larger_projection(0, t, h)
+        for step, (blk, t, h) in enumerate(units0):
+            larger = new_larger()
+            larger_projection(0, t, h, larger)
             if pending:
                 shortfall(*pending)
             pending = (short0[h], larger, 0, t, h * HALF, HALF)
-            if (t, h) == (2, 0):
-                grouped_a[0] = round_weight(a_raw[0, 1])
-            if (t, h) == (3, 0):
-                a_mx[0, 1] = quantise(grouped_a[0], "a01")
-                grouped_a[1] = round_weight(a_raw[1, 1])
-            if (t, h) == (3, 1):
-                a_mx[1, 1] = quantise(grouped_a[1], "a11")
-                grouped_h00 = clamp(short0[0], 0, HALF)
-
-        short1 = new_short()
-        for t in range(PACK):
-            larger = larger_projection(1, t, 0)
-            shortfall(*pending)
-            pending = (short1, larger, 1, t, 0, HALF)
-            if t == 0:
-                grouped_h01 = clamp(short0[1], HALF, HALF)
-            if t == 1:
-                h_mx[0, 0] = quantise(grouped_h00, "h00")
+            if step == 2:
+                contact_projections([(1, t, 0) for t in range(PACK)], "g00")
+                grouped_a01 = round_weight(a_raw[0, 1])
+            if step == 4:
+                grouped_a11 = round_weight(a_raw[1, 1])
+            if step == 6:
+                later_codes = codes_pair("a1_codes", "tab2_table")
+                later_scales = held_scales("a1_scales", 2)
+                a_mx[0, 1] = quantise(grouped_a01, "a01", later_codes[0], later_scales[0])
+                a_mx[1, 1] = quantise(grouped_a11, "a11", later_codes[1], later_scales[1])
+                contact_projections([(1, t, 1) for t in range(PACK)], "g02")
                 grouped_w0 = round_weight(w_raw[0])
-            if t == 2:
-                h_mx[0, 1] = quantise(grouped_h01, "h01")
-            if t == 3:
-                w_mx[0] = quantise(grouped_w0, "w0")
-                grouped_w1 = round_weight(w_raw[1])
-
-        short2 = new_short()
-        kept = []
-        for t in range(PACK):
-            larger = larger_projection(1, t, 1)
-            kept.append(larger)
-            shortfall(*pending)
-            pending = (short2, larger, 1, t) + CHUNKS[1]
-            if t == 0:
-                grouped_h10 = clamp(short1, 0, HALF)
-            if t == 2:
-                w_mx[1] = quantise(grouped_w1, "w1")
-            if t == 3:
-                h_mx[1, 0] = quantise(grouped_h10, "h10")
-                features(0, HALF, False)
+        grouped_h00 = clamp(short0[0])
+        grouped_w1 = round_weight(w_raw[1], "g01", 1)
         shortfall(*pending)
-        grouped_b = clamp(short2, *CHUNKS[1])
+        grouped_h01 = clamp(short0[1])
+
+        short1 = new_short(HALF)
+        pending = None
         for t in range(PACK):
-            shortfall(short2, kept[t], 1, t, *CHUNKS[2])
-            if t == 2:
-                h_mx[1, CHUNKS[1][0]] = quantise(grouped_b, "h11")
-                features(CHUNKS[1][0], CHUNKS[1][1], False)
-        grouped_c = clamp(short2, *CHUNKS[2])
-        h_mx[1, CHUNKS[2][0]] = quantise(grouped_c, "h12")
-        features(CHUNKS[2][0], CHUNKS[2][1], True)
+            larger = new_larger()
+            larger_projection(1, t, 0, larger)
+            if pending:
+                shortfall(*pending)
+            pending = (short1, larger, 1, t, 0, HALF)
+        late_codes = ring.tile([P, 4 * PASS], U32, name="late_codes", tag="g03", bufs=1, align_bytes=64)
+        late_scales = held_scales("w0_h00_scales", 2)
+        w_mx[0] = quantise(grouped_w0, "w0", late_codes[:, 0:PASS], late_scales[0])
+        h_mx[0, 0] = quantise(grouped_h00, "h00", late_codes[:, 2 * PASS : 3 * PASS], late_scales[1])
+        shortfall(*pending)
+        grouped_h10 = clamp(short1)
+        late_scales = held_scales("w1_h01_scales", 2)
+        h_mx[0, 1] = quantise(grouped_h01, "h01", late_codes[:, 3 * PASS : 4 * PASS], late_scales[1])
+        w_mx[1] = quantise(grouped_w1, "w1", late_codes[:, PASS : 2 * PASS], late_scales[0])
+
+        shorts = [new_short(count) for first, count in CHUNKS[:2]]
+        kept = ring.tile([P, PACK * HALF], F32, name="kept", tag="g01", bufs=1, align_bytes=64)
+        kept_of = [kept[:, t * HALF : (t + 1) * HALF] for t in range(PACK)]
+        for t in range(PACK):
+            larger_projection(1, t, 1, kept_of[t])
+            if t == 1:
+                h_mx[1, 0] = quantise(grouped_h10, "h10")
+            if t > 0:
+                shortfall(shorts[0], kept_of[t - 1], 1, t - 1, *CHUNKS[0])
+        shortfall(shorts[0], kept_of[PACK - 1], 1, PACK - 1, *CHUNKS[0])
+        grouped = clamp(shorts[0], tag="chunk0", bufs=1)
+        features_of_half()
+        last = len(CHUNKS) - 1
+        for n in range(1, last):
+            if n >= 2:
+                shorts.append(ring.tile([P, PACK, CHUNKS[n][1]], F32, name="short", tag="chunk%d" % (n - 2), align_bytes=64))
+            for t in range(PACK):
+                shortfall(shorts[n], kept_of[t], 1, t, *CHUNKS[n])
+            h_mx[1, CHUNKS[n - 1][0]] = quantise(grouped, "h1_%d" % n)
+            grouped = clamp(shorts[n], tag="chunk%d" % n, bufs=1)
+            features_of_chunk(*CHUNKS[n - 1])
+        first, count = CHUNKS[last]
+        grouped_last = keep.tile([P, PACK * count], BF16, name="grouped_last", align_bytes=64)
+        woven = grouped_last[:].rearrange("p (c t) -> p c t", t=PACK)
+        low = ring.tile([P, 2, count], F32, name="short", tag="chunk%d" % (last - 2), align_bytes=64)
+        for t in range(2):
+            shortfall(low, kept_of[t], 1, t, first, count)
+        nc.scalar.activation(out=woven[:, :, 0:2], in_=low[:].rearrange("p t c -> p c t"), func=ACT.Relu, scale=-1.0)
+        h_mx[1, CHUNKS[last - 1][0]] = quantise(grouped, "h1_before_last")
+        features_of_chunk(*CHUNKS[last - 1])
+        high = ring.tile([P, 2, count], F32, name="short", tag="chunk%d" % (last - 1), align_bytes=64)
+        for t in range(2, PACK):
+            shortfall(high, kept_of[t], 1, t, first, count)
+        nc.vector.tensor_scalar(woven[:, :, 2:PACK], high[:].rearrange("p t c -> p c t"), -1.0, 0.0, ALU.mult, ALU.max)
+        h_mx[1, first] = quantise(grouped_last, "h1_last")
+        features_of_last_chunk(first, count)

@@ -19,12 +19,19 @@ ACT = mybir.ActivationFunctionType
 P = 128
 PACK = 4
 PASS = P * PACK
-HALF = 512
+HALF = S // 2
 LANES = 16
+QUADS = 4
+LINE = 4
+
 RAW_BUFS = 5
 GROUPED_BUFS = 6
 LARGER_BUFS = 3
-CHUNKS = [(512, 128), (640, 128), (768, 128), (896, 128)]
+SHORT_BUFS = 3
+P_BANKS, Q_BANKS = 3, 5
+
+CHUNK = 128
+CHUNKS = [(first, CHUNK) for first in range(HALF, S, CHUNK)]
 
 
 def tile_list_residue_contact_max_kernel(
@@ -36,13 +43,20 @@ def tile_list_residue_contact_max_kernel(
         ring = ctx.enter_context(tc.tile_pool(name="ring", bufs=1))
         psum = ctx.enter_context(tc.psum_pool(name="psum", bufs=1))
 
-        def load_scale_rows(scales, name):
+
+        def load_list(source, name):
+            entries = keep.tile([P, S // LANES], U16, name=name)
+            nc.sync.dma_start(entries[:], source)
+            return entries
+
+        def load_plane(scales, name):
             passes, width = scales.shape[0], scales.shape[2]
-            plane = keep.tile([P, width], U8, name=name, align_bytes=64)
+            plane = ring.tile([P, width], U8, name=name, tag=name, align_bytes=64)
             nc.vector.memset(plane[:].bitcast(I32), 0)
-            for quad in range(4):
-                rows = scales[:, 4 * quad : 4 * quad + 4, :] if passes > 1 else scales[0, 4 * quad : 4 * quad + 4, :]
-                nc.sync.dma_start(plane[32 * quad : 32 * quad + 4 * passes, :].bitcast(I32), rows.bitcast(I32))
+            for quad in range(QUADS):
+                span = slice(PACK * quad, PACK * (quad + 1))
+                rows = scales[:, span, :] if passes > 1 else scales[0, span, :]
+                nc.sync.dma_start(plane[32 * quad : 32 * quad + PACK * passes, :].bitcast(I32), rows.bitcast(I32))
             return plane
 
         def load_words(words, name):
@@ -58,23 +72,21 @@ def tile_list_residue_contact_max_kernel(
         def load_thresholds(blk, t):
             name = "g%d%d" % (blk, t)
             rows = ring.tile([P, T], F32, name=name, tag=name, align_bytes=64)
-            nc.sync.dma_start(rows[:], gT[blk * PASS : (blk + 1) * PASS, :].rearrange("(p t) c -> p t c", t=PACK)[:, t, :])
+            nc.sync.dma_start(rows[:], gT[blk * PASS : (blk + 1) * PASS, :].rearrange("(m t) c -> m t c", t=PACK)[:, t, :])
             return rows
 
         a_raw, w_raw, g_rows = {}, {}, {}
         tab2_table = load_words(tab2_words[0], "tab2_table")
-        idx2 = keep.tile([P, S // LANES], U16, name="idx2")
-        nc.sync.dma_start(idx2[:], offs2)
-        tab2_plane = load_scale_rows(tab2_scales, "tab2_plane")
+        idx2 = load_list(offs2, "idx2")
+        tab2_plane = load_plane(tab2_scales, "tab2_plane")
         a_raw[0, 0] = load_weight(a[0:PASS, 0:PASS])
-        idx = keep.tile([P, S // LANES], U16, name="idx")
-        nc.sync.dma_start(idx[:], offs)
-        tab_plane = load_scale_rows(tab_scales, "tab_plane")
+        idx = load_list(offs, "idx")
+        tab_plane = load_plane(tab_scales, "tab_plane")
+        a_raw[1, 0] = load_weight(a[PASS:K, 0:PASS], "a10_raw", 1)
         b4_raw = keep.tile([P, 2 * H], U8, name="b4_raw", align_bytes=64)
         nc.sync.dma_start(b4_raw[:].bitcast(I32), b4_words[0].bitcast(I32))
-        b4_plane = load_scale_rows(b4_scales, "b4_plane")
+        b4_plane = load_plane(b4_scales, "b4_plane")
         tab_table0 = load_words(tab_words[0], "tab_table0")
-        a_raw[1, 0] = load_weight(a[PASS:K, 0:PASS], "a10_raw", 1)
         tab_table1 = load_words(tab_words[1], "tab_table1")
         g_rows[0, 0] = load_thresholds(0, 0)
         a_raw[0, 1] = load_weight(a[0:PASS, PASS:H])
@@ -83,22 +95,27 @@ def tile_list_residue_contact_max_kernel(
         g_rows[0, 2] = load_thresholds(0, 2)
         w_raw[0] = load_weight(w[0:PASS, :])
         g_rows[0, 3] = load_thresholds(0, 3)
-        w_raw[1] = load_weight(w[PASS:H, :])
         for t in range(PACK):
             g_rows[1, t] = load_thresholds(1, t)
+        w_raw[1] = load_weight(w[PASS:H, :])
         bias_cols = keep.tile([P, PACK], F32, name="bias_cols")
-        nc.sync.dma_start(bias_cols[:], bias.rearrange("(p t) -> p t", t=PACK))
+        nc.sync.dma_start(bias_cols[:], bias.rearrange("(m t) -> m t", t=PACK))
 
-        def offsets(lst, first, count):
-            return lst[:, first // LANES : (first + count) // LANES]
 
-        def pick(window, lst, half, dtype, name):
-            picked = keep.tile([P, HALF], dtype, name="%s_%d" % (name, half), align_bytes=64)
-            nc.vector.tensor_copy(picked[:], window.indirect(offsets(lst, half * HALF, HALF)))
+        def offsets(entries, first, count):
+            return entries[:, first // LANES : (first + count) // LANES]
+
+        def pick(window, entries, first, count, dtype, name):
+            picked = keep.tile([P, count], dtype, name=name, align_bytes=64)
+            nc.vector.tensor_copy(picked[:], window.indirect(offsets(entries, first, count)))
             return picked
 
-        def round_weight(raw, tag="grouped", bufs=GROUPED_BUFS):
-            grouped = ring.tile([P, PACK * PASS], BF16, name="grouped", tag=tag, bufs=bufs, align_bytes=64)
+        def pick_halves(window, entries, dtype, name):
+            picked = pick(window, entries, 0, S, dtype, name)
+            return [picked[:, half * HALF : (half + 1) * HALF] for half in range(2)]
+
+        def round_weight(raw):
+            grouped = ring.tile([P, PACK * PASS], BF16, name="grouped", tag="grouped", bufs=GROUPED_BUFS, align_bytes=64)
             nc.scalar.copy(
                 out=grouped[:].rearrange("p (t m i) -> p m i t", t=PACK, i=PACK),
                 in_=raw[:].rearrange("p i (m t) -> p m i t", t=PACK),
@@ -114,101 +131,102 @@ def tile_list_residue_contact_max_kernel(
             nc.vector.quantize_mx(out=codes.bitcast(FP8X4), scales=scales, in_=grouped[:])
             return codes, scales
 
-        def held_scales(name, count):
+        def codes_in_slot(name, count, tag):
+            words = ring.tile([P, count * PASS], U32, name=name, tag=tag, align_bytes=64)
+            return [words[:, n * PASS : (n + 1) * PASS] for n in range(count)]
+
+        def planes_in_larger_slot(name, count):
             planes = ring.tile([P, count * PASS], U8, name=name, tag="larger", bufs=LARGER_BUFS, align_bytes=64)
             return [planes[:, n * PASS : (n + 1) * PASS] for n in range(count)]
 
-        def codes_pair(name, tag):
-            pair = ring.tile([P, 2 * PASS], U32, name=name, tag=tag, align_bytes=64)
-            return pair[:, 0:PASS], pair[:, PASS : 2 * PASS]
-
-        v2_scales = [pick(tab2_plane[:], idx2, h, U8, "v2_scales") for h in range(2)]
-        v2_words = [pick(tab2_table[:].bitcast(U32), idx2, h, U32, "v2_words") for h in range(2)]
+        v2_scales = pick_halves(tab2_plane[:], idx2, U8, "v2_scales")
+        v2_words = pick_halves(tab2_table[:].bitcast(U32), idx2, U32, "v2_words")
         a_mx, w_mx, h_mx = {}, {}, {}
-        grouped_a00 = round_weight(a_raw[0, 0])
-        grouped_a10 = round_weight(a_raw[1, 0])
-        v_scales = [pick(tab_plane[:], idx, h, U8, "v_scales") for h in range(2)]
-        v_words = {(0, h): pick(tab_table0[:].bitcast(U32), idx, h, U32, "v_words0") for h in range(2)}
-        first_codes = codes_pair("a0_codes", "tab_table0")
-        a_mx[0, 0] = quantise(grouped_a00, "a00", first_codes[0])
+        a_grouped = {(c, 0): round_weight(a_raw[c, 0]) for c in range(2)}
+        v_scales = pick_halves(tab_plane[:], idx, U8, "v_scales")
+        v_words = [pick_halves(tab_table0[:].bitcast(U32), idx, U32, "v_words0")]
+        a0_codes = codes_in_slot("a0_codes", 2, "tab_plane")
+        a_mx[0, 0] = quantise(a_grouped[0, 0], "a00", a0_codes[0])
 
         b4_codes = keep.tile([P, 2 * H], U8, name="b4_codes", align_bytes=64)
         nc.vector.tensor_copy(
             out=b4_codes[:].bitcast(U16).rearrange("p (b t m) -> p b t m", t=PACK, m=P),
             in_=b4_raw[:].bitcast(U16).rearrange("p (b m t) -> p b t m", t=PACK, m=P),
         )
-        b4_dealt = keep.tile([P, H], U8, name="b4_dealt", align_bytes=64)
+        b4_dealt_plane = keep.tile([P, H], U8, name="b4_dealt_plane", align_bytes=64)
         nc.vector.tensor_copy(
-            out=b4_dealt[:].rearrange("p (b t m) -> p b t m", t=PACK, m=P),
+            out=b4_dealt_plane[:].rearrange("p (b t m) -> p b t m", t=PACK, m=P),
             in_=b4_plane[:].rearrange("p (b m t) -> p b t m", t=PACK, m=P),
         )
-        a_mx[1, 0] = quantise(grouped_a10, "a10", first_codes[1])
-        v_words[1, 0] = pick(tab_table1[:].bitcast(U32), idx, 0, U32, "v_words1")
-        v_words[1, 1] = pick(tab_table1[:].bitcast(U32), idx, 1, U32, "v_words1")
+        a_mx[1, 0] = quantise(a_grouped[1, 0], "a10", a0_codes[1])
+        v_words.append(
+            [pick(tab_table1[:].bitcast(U32), idx, half * HALF, HALF, U32, "v_words1_%d" % half)[:] for half in range(2)]
+        )
+
+
+        q_of = {}
 
         def contact_projections(units, tag):
             q_rows = ring.tile([P, len(units) * HALF], F32, name="q_rows", tag=tag, align_bytes=64)
             for n, (blk, t, half) in enumerate(units):
-                first = blk * PASS + t * P
-                q_acc = psum.tile([P, HALF], F32, name="q_acc", tag="q", bufs=2)
+                col = blk * PASS + t * P
+                q_acc = psum.tile([P, HALF], F32, name="q_acc", tag="q", bufs=Q_BANKS)
                 nc.tensor.matmul_mx(
                     q_acc[:],
-                    lhsT=b4_codes[:, 2 * first : 2 * (first + P)].bitcast(FP4X4),
-                    lhsT_scale=b4_dealt[:, first : first + P],
-                    rhs=v2_words[half][:].bitcast(FP8X4),
-                    rhs_scale=v2_scales[half][:],
+                    lhsT=b4_codes[:, 2 * col : 2 * (col + P)].bitcast(FP4X4),
+                    lhsT_scale=b4_dealt_plane[:, col : col + P],
+                    rhs=v2_words[half].bitcast(FP8X4),
+                    rhs_scale=v2_scales[half],
                     start=True,
                     stop=True,
                 )
-                nc.scalar.copy(out=q_rows[:, n * HALF : (n + 1) * HALF], in_=q_acc[:])
                 q_of[blk, t, half] = q_rows[:, n * HALF : (n + 1) * HALF]
+                nc.scalar.copy(out=q_of[blk, t, half], in_=q_acc[:])
 
         def larger_projection(blk, t, half, larger):
             cols = slice(t * P, (t + 1) * P)
-            p_acc = psum.tile([P, HALF], F32, name="p_acc", tag="p", bufs=3)
+            p_acc = psum.tile([P, HALF], F32, name="p_acc", tag="p", bufs=P_BANKS)
             for c in range(2):
                 codes, scales = a_mx[c, blk]
                 nc.tensor.matmul_mx(
                     p_acc[:],
                     lhsT=codes[:, cols].bitcast(FP8X4),
                     lhsT_scale=scales[:, cols],
-                    rhs=v_words[c, half][:].bitcast(FP8X4),
-                    rhs_scale=v_scales[half][4 * c : P, :],
+                    rhs=v_words[c][half].bitcast(FP8X4),
+                    rhs_scale=v_scales[half][PACK * c : P, :],
                     start=(c == 0),
                     stop=(c == 1),
                 )
             nc.vector.tensor_tensor(larger, p_acc[:], q_of[blk, t, half], ALU.max)
 
-        def new_larger(tag="larger", bufs=LARGER_BUFS):
-            larger = ring.tile([P, HALF], F32, name="larger", tag=tag, bufs=bufs, align_bytes=64)
+        def new_larger():
+            larger = ring.tile([P, HALF], F32, name="larger", tag="larger", bufs=LARGER_BUFS, align_bytes=64)
             return larger[:]
 
         def new_short(count):
-            return ring.tile([P, PACK, count], F32, name="short", tag="short", bufs=3)
+            return ring.tile([P, PACK, count], F32, name="short", tag="short", bufs=SHORT_BUFS)
 
-        def shortfall(short, larger, blk, t, first, count):
+        def shortfall(row, larger, blk, t, first, count):
             lo = first % HALF
             nc.vector.tensor_tensor(
-                short[:, t % short.shape[1], :],
-                g_rows[blk, t][:].indirect(offsets(idx, first, count)),
-                larger[:, lo : lo + count],
-                ALU.subtract,
+                row, g_rows[blk, t][:].indirect(offsets(idx, first, count)), larger[:, lo : lo + count], ALU.subtract
             )
 
         def clamp(short, tag="grouped", bufs=GROUPED_BUFS):
             count = short.shape[2]
             grouped = ring.tile([P, PACK * count], BF16, name="grouped", tag=tag, bufs=bufs, align_bytes=64)
-            woven = grouped[:].rearrange("p (c i t) -> p c t i", t=PACK, i=4)
-            slices = short[:].rearrange("p t (c i) -> p c t i", i=4)
+            woven = grouped[:].rearrange("p (c i t) -> p c t i", t=PACK, i=LINE)
+            slices = short[:].rearrange("p t (c i) -> p c t i", i=LINE)
             nc.scalar.activation(out=woven, in_=slices, func=ACT.Relu, scale=-1.0)
             return grouped
 
-        out_rows = out.rearrange("(p t) j -> p t j", t=PACK)
+
+        out_rows = out.rearrange("(m t) j -> m t j", t=PACK)
 
         def feature_sums(y_acc, t, first, count):
-            half, lo = divmod(first, HALF)
+            lo = first % HALF
             cols = slice(t * P, (t + 1) * P)
-            operands = [(h_mx[0, half], slice(lo, lo + count)), (h_mx[1, first], slice(0, count))]
+            operands = [(h_mx[0, first - lo], slice(lo, lo + count)), (h_mx[1, first], slice(0, count))]
             for blk, ((codes, scales), span) in enumerate(operands):
                 nc.tensor.matmul_mx(
                     y_acc,
@@ -229,61 +247,35 @@ def tile_list_residue_contact_max_kernel(
         def new_staged(count):
             return ring.tile([P, PACK, count], F32, name="staged", tag="raw", bufs=RAW_BUFS, align_bytes=64)
 
-        def features_of_half():
-            staged = new_staged(HALF)
-            for t in range(PACK):
-                y_acc = psum.tile([P, HALF], F32, name="y_acc", tag="y", bufs=3)
-                feature_sums(y_acc[:], t, 0, HALF)
-                add_bias(staged, y_acc[:], t)
-                nc.sync.dma_start(out_rows[:, t, 0:HALF], staged[:, t, :])
 
-        def features_of_chunk(first, count):
-            staged = new_staged(count)
-            y_acc = psum.tile([P, PACK, count], F32, name="y_acc", tag="y", bufs=3)
-            for t in range(PACK):
-                feature_sums(y_acc[:, t, :], t, first, count)
-            for t in range(PACK):
-                add_bias(staged, y_acc[:, t, :], t)
-            nc.sync.dma_start(out_rows[:, :, first : first + count], staged[:])
+        units = [(0, t, half) for t in range(PACK) for half in range(2)]
+        contact_projections(units[:PACK], "a10_raw")
+        contact_projections(units[PACK:], "tab_table1")
 
-        def features_of_last_chunk(first, count):
-            staged = new_staged(count)
-            for t in range(PACK):
-                tag, bufs = (("p", 3), ("q", 2))[t // 2]
-                y_acc = psum.tile([P, count], F32, name="y_acc", tag=tag, bufs=bufs)
-                feature_sums(y_acc[:], t, first, count)
-                add_bias(staged, y_acc[:], t, on_vector=t % 2 == 0)
-            nc.sync.dma_start(out_rows[:, :, first : first + count], staged[:])
-
-        q_of = {}
-        units0 = [(0, t, h) for t in range(PACK) for h in range(2)]
-        contact_projections(units0[:4], "a10_raw")
-        contact_projections(units0[4:], "tab_table1")
-
-        short0 = [new_short(HALF) for h in range(2)]
+        short0 = [new_short(HALF) for half in range(2)]
         pending = None
-        for step, (blk, t, h) in enumerate(units0):
+        for blk, t, half in units:
             larger = new_larger()
-            larger_projection(0, t, h, larger)
+            larger_projection(blk, t, half, larger)
             if pending:
                 shortfall(*pending)
-            pending = (short0[h], larger, 0, t, h * HALF, HALF)
-            if step == 2:
-                contact_projections([(1, t, 0) for t in range(PACK)], "g00")
-                grouped_a01 = round_weight(a_raw[0, 1])
-            if step == 4:
-                grouped_a11 = round_weight(a_raw[1, 1])
-            if step == 6:
-                later_codes = codes_pair("a1_codes", "tab2_table")
-                later_scales = held_scales("a1_scales", 2)
-                a_mx[0, 1] = quantise(grouped_a01, "a01", later_codes[0], later_scales[0])
-                a_mx[1, 1] = quantise(grouped_a11, "a11", later_codes[1], later_scales[1])
-                contact_projections([(1, t, 1) for t in range(PACK)], "g02")
-                grouped_w0 = round_weight(w_raw[0])
-        grouped_h00 = clamp(short0[0])
-        grouped_w1 = round_weight(w_raw[1], "g01", 1)
+            pending = (short0[half][:, t, :], larger, blk, t, half * HALF, HALF)
+            if (t, half) == (1, 0):
+                contact_projections([(1, s, 0) for s in range(PACK)], "g00")
+                a_grouped[0, 1] = round_weight(a_raw[0, 1])
+            if (t, half) == (2, 0):
+                a_grouped[1, 1] = round_weight(a_raw[1, 1])
+            if (t, half) == (3, 0):
+                a1_codes = codes_in_slot("a1_codes", 2, "tab2_table")
+                a1_planes = planes_in_larger_slot("a1_scales", 2)
+                for c in range(2):
+                    a_mx[c, 1] = quantise(a_grouped[c, 1], "a%d1" % c, a1_codes[c], a1_planes[c])
+                contact_projections([(1, s, 1) for s in range(PACK)], "g02")
+                w0_grouped = round_weight(w_raw[0])
+        h0_grouped = [clamp(short0[0])]
         shortfall(*pending)
-        grouped_h01 = clamp(short0[1])
+        h0_grouped.append(clamp(short0[1], "g01", 1))
+
 
         short1 = new_short(HALF)
         pending = None
@@ -292,50 +284,90 @@ def tile_list_residue_contact_max_kernel(
             larger_projection(1, t, 0, larger)
             if pending:
                 shortfall(*pending)
-            pending = (short1, larger, 1, t, 0, HALF)
-        late_codes = ring.tile([P, 4 * PASS], U32, name="late_codes", tag="g03", bufs=1, align_bytes=64)
-        late_scales = held_scales("w0_h00_scales", 2)
-        w_mx[0] = quantise(grouped_w0, "w0", late_codes[:, 0:PASS], late_scales[0])
-        h_mx[0, 0] = quantise(grouped_h00, "h00", late_codes[:, 2 * PASS : 3 * PASS], late_scales[1])
+            pending = (short1[:, t, :], larger, 1, t, 0, HALF)
+        w0_codes, w1_codes, h00_codes, h01_codes = codes_in_slot("late_codes", 4, "g03")
+        w0_plane, h00_plane = planes_in_larger_slot("w0_h00_scales", 2)
+        w_mx[0] = quantise(w0_grouped, "w0", w0_codes, w0_plane)
+        h_mx[0, 0] = quantise(h0_grouped[0], "h00", h00_codes, h00_plane)
         shortfall(*pending)
-        grouped_h10 = clamp(short1)
-        late_scales = held_scales("w1_h01_scales", 2)
-        h_mx[0, 1] = quantise(grouped_h01, "h01", late_codes[:, 3 * PASS : 4 * PASS], late_scales[1])
-        w_mx[1] = quantise(grouped_w1, "w1", late_codes[:, PASS : 2 * PASS], late_scales[0])
+        h10_grouped = clamp(short1)
+        h_mx[0, HALF] = quantise(h0_grouped[1], "h01", h01_codes, planes_in_larger_slot("h01_scales", 1)[0])
 
-        shorts = [new_short(count) for first, count in CHUNKS[:2]]
+        w1_grouped = []
+        for u, round_copy in enumerate((nc.vector.tensor_copy, nc.scalar.copy)):
+            w1_grouped.append(keep.tile([P, 2 * PASS], BF16, name="w1_grouped%d" % u, align_bytes=64))
+            round_copy(
+                out=w1_grouped[u][:].rearrange("p (t m i) -> p m i t", t=2, i=PACK),
+                in_=w_raw[1][:].rearrange("p i (m t) -> p m i t", t=PACK)[:, :, :, 2 * u : 2 * u + 2],
+            )
+        w1_plane = keep.tile([P, PASS], U8, name="w1_scales", align_bytes=64)
+        w_mx[1] = (w1_codes, w1_plane[:])
+
+        def quantise_w1(u):
+            cols = slice(2 * P * u, 2 * P * (u + 1))
+            quantise(w1_grouped[u], "w1", w1_codes[:, cols], w1_plane[:, cols])
+
+
+        shorts = [new_short(CHUNK) for n in range(2)]
         kept = ring.tile([P, PACK * HALF], F32, name="kept", tag="g01", bufs=1, align_bytes=64)
         kept_of = [kept[:, t * HALF : (t + 1) * HALF] for t in range(PACK)]
         for t in range(PACK):
             larger_projection(1, t, 1, kept_of[t])
+            if t == 0:
+                quantise_w1(0)
             if t == 1:
-                h_mx[1, 0] = quantise(grouped_h10, "h10")
+                h_mx[1, 0] = quantise(h10_grouped, "h10")
+            if t == 2:
+                quantise_w1(1)
             if t > 0:
-                shortfall(shorts[0], kept_of[t - 1], 1, t - 1, *CHUNKS[0])
-        shortfall(shorts[0], kept_of[PACK - 1], 1, PACK - 1, *CHUNKS[0])
-        grouped = clamp(shorts[0], tag="chunk0", bufs=1)
-        features_of_half()
+                shortfall(shorts[0][:, t - 1, :], kept_of[t - 1], 1, t - 1, *CHUNKS[0])
+        shortfall(shorts[0][:, PACK - 1, :], kept_of[PACK - 1], 1, PACK - 1, *CHUNKS[0])
+
+        grouped = clamp(shorts[0], "chunk0", 1)
         last = len(CHUNKS) - 1
         for n in range(1, last):
             if n >= 2:
-                shorts.append(ring.tile([P, PACK, CHUNKS[n][1]], F32, name="short", tag="chunk%d" % (n - 2), align_bytes=64))
+                shorts.append(ring.tile([P, PACK, CHUNK], F32, name="short", tag="chunk%d" % (n - 2), align_bytes=64))
             for t in range(PACK):
-                shortfall(shorts[n], kept_of[t], 1, t, *CHUNKS[n])
-            h_mx[1, CHUNKS[n - 1][0]] = quantise(grouped, "h1_%d" % n)
-            grouped = clamp(shorts[n], tag="chunk%d" % n, bufs=1)
-            features_of_chunk(*CHUNKS[n - 1])
-        first, count = CHUNKS[last]
-        grouped_last = keep.tile([P, PACK * count], BF16, name="grouped_last", align_bytes=64)
-        woven = grouped_last[:].rearrange("p (c t) -> p c t", t=PACK)
-        low = ring.tile([P, 2, count], F32, name="short", tag="chunk%d" % (last - 2), align_bytes=64)
+                shortfall(shorts[n][:, t, :], kept_of[t], 1, t, *CHUNKS[n])
+            h_mx[1, CHUNKS[n - 1][0]] = quantise(grouped, "h1_%d" % (n - 1))
+            grouped = clamp(shorts[n], "chunk%d" % n, 1)
+
+        first = CHUNKS[last][0]
+        last_grouped = keep.tile([P, PACK * CHUNK], BF16, name="last_grouped", align_bytes=64)
+        last_woven = last_grouped[:].rearrange("p (c t) -> p c t", t=PACK)
+        low = ring.tile([P, 2, CHUNK], F32, name="short", tag="chunk%d" % (last - 2), align_bytes=64)
         for t in range(2):
-            shortfall(low, kept_of[t], 1, t, first, count)
-        nc.scalar.activation(out=woven[:, :, 0:2], in_=low[:].rearrange("p t c -> p c t"), func=ACT.Relu, scale=-1.0)
-        h_mx[1, CHUNKS[last - 1][0]] = quantise(grouped, "h1_before_last")
-        features_of_chunk(*CHUNKS[last - 1])
-        high = ring.tile([P, 2, count], F32, name="short", tag="chunk%d" % (last - 1), align_bytes=64)
+            shortfall(low[:, t, :], kept_of[t], 1, t, first, CHUNK)
+        nc.scalar.activation(out=last_woven[:, :, 0:2], in_=low[:].rearrange("p t c -> p c t"), func=ACT.Relu, scale=-1.0)
+        h_mx[1, CHUNKS[last - 1][0]] = quantise(grouped, "h1_%d" % (last - 1))
+        high = ring.tile([P, 2, CHUNK], F32, name="short", tag="chunk%d" % (last - 1), align_bytes=64)
         for t in range(2, PACK):
-            shortfall(high, kept_of[t], 1, t, first, count)
-        nc.vector.tensor_scalar(woven[:, :, 2:PACK], high[:].rearrange("p t c -> p c t"), -1.0, 0.0, ALU.mult, ALU.max)
-        h_mx[1, first] = quantise(grouped_last, "h1_last")
-        features_of_last_chunk(first, count)
+            shortfall(high[:, t - 2, :], kept_of[t], 1, t, first, CHUNK)
+        nc.vector.tensor_scalar(last_woven[:, :, 2:PACK], high[:].rearrange("p t c -> p c t"), -1.0, 0.0, ALU.mult, ALU.max)
+        h_mx[1, first] = quantise(last_grouped, "h1_%d" % last)
+
+
+        staged = new_staged(HALF)
+        for t in range(PACK):
+            y_acc = psum.tile([P, HALF], F32, name="y_acc", tag="q", bufs=Q_BANKS)
+            feature_sums(y_acc[:], t, 0, HALF)
+            add_bias(staged, y_acc[:], t)
+            nc.sync.dma_start(out_rows[:, t, 0:HALF], staged[:, t, :])
+
+        for start, count in CHUNKS[:last]:
+            staged = new_staged(count)
+            y_acc = psum.tile([P, PACK, count], F32, name="y_acc", tag="q", bufs=Q_BANKS)
+            for t in range(PACK):
+                feature_sums(y_acc[:, t, :], t, start, count)
+            for t in range(PACK):
+                add_bias(staged, y_acc[:, t, :], t)
+            nc.sync.dma_start(out_rows[:, :, start : start + count], staged[:])
+
+        staged = new_staged(CHUNK)
+        for t in range(PACK):
+            tag, bufs = ("p", P_BANKS) if t < P_BANKS else ("q", Q_BANKS)
+            y_acc = psum.tile([P, CHUNK], F32, name="y_acc", tag=tag, bufs=bufs)
+            feature_sums(y_acc[:], t, first, CHUNK)
+            add_bias(staged, y_acc[:], t, on_vector=t % 2 == 0)
+        nc.sync.dma_start(out_rows[:, :, first : first + CHUNK], staged[:])

@@ -79,12 +79,12 @@ def tile_list_residue_contact_max_kernel(
         tab2_table = load_words(tab2_words[0], "tab2_table")
         idx2 = load_list(offs2, "idx2")
         tab2_plane = load_plane(tab2_scales, "tab2_plane")
+        b4_raw = keep.tile([P, 2 * H], U8, name="b4_raw", align_bytes=64)
+        nc.sync.dma_start(b4_raw[:].bitcast(I32), b4_words[0].bitcast(I32))
         a_raw[0, 0] = load_weight(a[0:PASS, 0:PASS])
         idx = load_list(offs, "idx")
         tab_plane = load_plane(tab_scales, "tab_plane")
         a_raw[1, 0] = load_weight(a[PASS:K, 0:PASS], "a10_raw", 1)
-        b4_raw = keep.tile([P, 2 * H], U8, name="b4_raw", align_bytes=64)
-        nc.sync.dma_start(b4_raw[:].bitcast(I32), b4_words[0].bitcast(I32))
         b4_plane = load_plane(b4_scales, "b4_plane")
         tab_table0 = load_words(tab_words[0], "tab_table0")
         tab_table1 = load_words(tab_words[1], "tab_table1")
@@ -95,9 +95,9 @@ def tile_list_residue_contact_max_kernel(
         g_rows[0, 2] = load_thresholds(0, 2)
         w_raw[0] = load_weight(w[0:PASS, :])
         g_rows[0, 3] = load_thresholds(0, 3)
+        w_raw[1] = load_weight(w[PASS:H, :])
         for t in range(PACK):
             g_rows[1, t] = load_thresholds(1, t)
-        w_raw[1] = load_weight(w[PASS:H, :])
         bias_cols = keep.tile([P, PACK], F32, name="bias_cols")
         nc.sync.dma_start(bias_cols[:], bias.rearrange("(m t) -> m t", t=PACK))
 
@@ -114,8 +114,8 @@ def tile_list_residue_contact_max_kernel(
             picked = pick(window, entries, 0, S, dtype, name)
             return [picked[:, half * HALF : (half + 1) * HALF] for half in range(2)]
 
-        def round_weight(raw):
-            grouped = ring.tile([P, PACK * PASS], BF16, name="grouped", tag="grouped", bufs=GROUPED_BUFS, align_bytes=64)
+        def round_weight(raw, tag="grouped", bufs=GROUPED_BUFS):
+            grouped = ring.tile([P, PACK * PASS], BF16, name="grouped", tag=tag, bufs=bufs, align_bytes=64)
             nc.scalar.copy(
                 out=grouped[:].rearrange("p (t m i) -> p m i t", t=PACK, i=PACK),
                 in_=raw[:].rearrange("p i (m t) -> p m i t", t=PACK),
@@ -149,12 +149,12 @@ def tile_list_residue_contact_max_kernel(
         a_mx[0, 0] = quantise(a_grouped[0, 0], "a00", a0_codes[0])
 
         b4_codes = keep.tile([P, 2 * H], U8, name="b4_codes", align_bytes=64)
-        nc.vector.tensor_copy(
-            out=b4_codes[:].bitcast(U16).rearrange("p (b t m) -> p b t m", t=PACK, m=P),
-            in_=b4_raw[:].bitcast(U16).rearrange("p (b m t) -> p b t m", t=PACK, m=P),
+        nc.gpsimd.tensor_copy(
+            out=b4_codes[:].rearrange("p (b t m e) -> p b t m e", t=PACK, m=P, e=2),
+            in_=b4_raw[:].rearrange("p (b m t e) -> p b t m e", t=PACK, m=P, e=2),
         )
         b4_dealt_plane = keep.tile([P, H], U8, name="b4_dealt_plane", align_bytes=64)
-        nc.vector.tensor_copy(
+        nc.gpsimd.tensor_copy(
             out=b4_dealt_plane[:].rearrange("p (b t m) -> p b t m", t=PACK, m=P),
             in_=b4_plane[:].rearrange("p (b m t) -> p b t m", t=PACK, m=P),
         )
@@ -273,8 +273,9 @@ def tile_list_residue_contact_max_kernel(
                 contact_projections([(1, s, 1) for s in range(PACK)], "g02")
                 w0_grouped = round_weight(w_raw[0])
         h0_grouped = [clamp(short0[0])]
+        w1_grouped = round_weight(w_raw[1], "g01", 1)
         shortfall(*pending)
-        h0_grouped.append(clamp(short0[1], "g01", 1))
+        h0_grouped.append(clamp(short0[1]))
 
 
         short1 = new_short(HALF)
@@ -291,21 +292,9 @@ def tile_list_residue_contact_max_kernel(
         h_mx[0, 0] = quantise(h0_grouped[0], "h00", h00_codes, h00_plane)
         shortfall(*pending)
         h10_grouped = clamp(short1)
-        h_mx[0, HALF] = quantise(h0_grouped[1], "h01", h01_codes, planes_in_larger_slot("h01_scales", 1)[0])
-
-        w1_grouped = []
-        for u, round_copy in enumerate((nc.vector.tensor_copy, nc.scalar.copy)):
-            w1_grouped.append(keep.tile([P, 2 * PASS], BF16, name="w1_grouped%d" % u, align_bytes=64))
-            round_copy(
-                out=w1_grouped[u][:].rearrange("p (t m i) -> p m i t", t=2, i=PACK),
-                in_=w_raw[1][:].rearrange("p i (m t) -> p m i t", t=PACK)[:, :, :, 2 * u : 2 * u + 2],
-            )
-        w1_plane = keep.tile([P, PASS], U8, name="w1_scales", align_bytes=64)
-        w_mx[1] = (w1_codes, w1_plane[:])
-
-        def quantise_w1(u):
-            cols = slice(2 * P * u, 2 * P * (u + 1))
-            quantise(w1_grouped[u], "w1", w1_codes[:, cols], w1_plane[:, cols])
+        w1_plane, h01_plane = planes_in_larger_slot("w1_h01_scales", 2)
+        h_mx[0, HALF] = quantise(h0_grouped[1], "h01", h01_codes, h01_plane)
+        w_mx[1] = quantise(w1_grouped, "w1", w1_codes, w1_plane)
 
 
         shorts = [new_short(CHUNK) for n in range(2)]
@@ -313,12 +302,8 @@ def tile_list_residue_contact_max_kernel(
         kept_of = [kept[:, t * HALF : (t + 1) * HALF] for t in range(PACK)]
         for t in range(PACK):
             larger_projection(1, t, 1, kept_of[t])
-            if t == 0:
-                quantise_w1(0)
             if t == 1:
                 h_mx[1, 0] = quantise(h10_grouped, "h10")
-            if t == 2:
-                quantise_w1(1)
             if t > 0:
                 shortfall(shorts[0][:, t - 1, :], kept_of[t - 1], 1, t - 1, *CHUNKS[0])
         shortfall(shorts[0][:, PACK - 1, :], kept_of[PACK - 1], 1, PACK - 1, *CHUNKS[0])

from contextlib import ExitStack

import concourse.mybir as mybir

K, L, H, N, T, S = 1024, 512, 1024, 512, 2048, 1024
FLOPS = 2 * S * (K * H + L * H + H * N)

F32 = mybir.dt.float32
BF16 = mybir.dt.bfloat16
I32 = mybir.dt.int32
U32 = mybir.dt.uint32
U16 = mybir.dt.uint16
U8 = mybir.dt.uint8
FP8X4 = mybir.dt.float8_e4m3fn_x4
FP4X4 = mybir.dt.float4_e2m1fn_x4
ALU = mybir.AluOpType
ACT = mybir.ActivationFunctionType

P = 128
PACK = 4
PASS = P * PACK
HALF = S // 2
LANES = 16
QUADS = 4
LINE = 4

RAW_BUFS = 5
GROUPED_BUFS = 6
LARGER_BUFS = 3
SHORT_BUFS = 3
P_BANKS, Q_BANKS = 3, 5

CHUNK = 128
CHUNKS = [(first, CHUNK) for first in range(HALF, S, CHUNK)]


def tile_list_residue_contact_max_kernel(
    tc, tab_words, tab_scales, tab2_words, tab2_scales, offs, offs2, a, b4_words, b4_scales, gT, w, bias, out
):
    nc = tc.nc
    with ExitStack() as ctx:
        keep = ctx.enter_context(tc.tile_pool(name="keep", bufs=1))
        ring = ctx.enter_context(tc.tile_pool(name="ring", bufs=1))
        psum = ctx.enter_context(tc.psum_pool(name="psum", bufs=1))


        def load_list(source, name):
            entries = keep.tile([P, S // LANES], U16, name=name)
            nc.sync.dma_start(entries[:], source)
            return entries

        def load_plane(scales, name):
            passes, width = scales.shape[0], scales.shape[2]
            plane = ring.tile([P, width], U8, name=name, tag=name, align_bytes=64)
            nc.vector.memset(plane[:].bitcast(I32), 0)
            for quad in range(QUADS):
                span = slice(PACK * quad, PACK * (quad + 1))
                rows = scales[:, span, :] if passes > 1 else scales[0, span, :]
                nc.sync.dma_start(plane[32 * quad : 32 * quad + PACK * passes, :].bitcast(I32), rows.bitcast(I32))
            return plane

        def load_words(words, name):
            table = ring.tile([P, T], I32, name=name, tag=name, align_bytes=64)
            nc.sync.dma_start(table[:], words.rearrange("p n i -> p (n i)").bitcast(I32))
            return table

        def load_weight(rows, tag="raw", bufs=RAW_BUFS):
            raw = ring.tile([P, PACK, PASS], F32, name="raw", tag=tag, bufs=bufs, align_bytes=64)
            nc.sync.dma_start(raw[:], rows.rearrange("(p i) c -> p i c", i=PACK))
            return raw

        def load_thresholds(blk, t):
            name = "g%d%d" % (blk, t)
            rows = ring.tile([P, T], F32, name=name, tag=name, align_bytes=64)
            nc.sync.dma_start(rows[:], gT[blk * PASS : (blk + 1) * PASS, :].rearrange("(m t) c -> m t c", t=PACK)[:, t, :])
            return rows

        a_raw, w_raw, g_rows = {}, {}, {}
        tab2_table = load_words(tab2_words[0], "tab2_table")
        idx2 = load_list(offs2, "idx2")
        tab2_plane = load_plane(tab2_scales, "tab2_plane")
        b4_raw = keep.tile([P, 2 * H], U8, name="b4_raw", align_bytes=64)
        nc.sync.dma_start(b4_raw[:].bitcast(I32), b4_words[0].bitcast(I32))
        a_raw[0, 0] = load_weight(a[0:PASS, 0:PASS])
        idx = load_list(offs, "idx")
        tab_plane = load_plane(tab_scales, "tab_plane")
        a_raw[1, 0] = load_weight(a[PASS:K, 0:PASS], "a10_raw", 1)
        b4_plane = load_plane(b4_scales, "b4_plane")
        tab_table0 = load_words(tab_words[0], "tab_table0")
        tab_table1 = load_words(tab_words[1], "tab_table1")
        g_rows[0, 0] = load_thresholds(0, 0)
        a_raw[0, 1] = load_weight(a[0:PASS, PASS:H])
        g_rows[0, 1] = load_thresholds(0, 1)
        a_raw[1, 1] = load_weight(a[PASS:K, PASS:H])
        g_rows[0, 2] = load_thresholds(0, 2)
        w_raw[0] = load_weight(w[0:PASS, :])
        g_rows[0, 3] = load_thresholds(0, 3)
        w_raw[1] = load_weight(w[PASS:H, :])
        for t in range(PACK):
            g_rows[1, t] = load_thresholds(1, t)
        bias_cols = keep.tile([P, PACK], F32, name="bias_cols")
        nc.sync.dma_start(bias_cols[:], bias.rearrange("(m t) -> m t", t=PACK))


        def offsets(entries, first, count):
            return entries[:, first // LANES : (first + count) // LANES]

        def pick(window, entries, first, count, dtype, name):
            picked = keep.tile([P, count], dtype, name=name, align_bytes=64)
            nc.vector.tensor_copy(picked[:], window.indirect(offsets(entries, first, count)))
            return picked

        def pick_halves(window, entries, dtype, name):
            picked = pick(window, entries, 0, S, dtype, name)
            return [picked[:, half * HALF : (half + 1) * HALF] for half in range(2)]

        def round_weight(raw, tag="grouped", bufs=GROUPED_BUFS):
            grouped = ring.tile([P, PACK * PASS], BF16, name="grouped", tag=tag, bufs=bufs, align_bytes=64)
            nc.scalar.copy(
                out=grouped[:].rearrange("p (t m i) -> p m i t", t=PACK, i=PACK),
                in_=raw[:].rearrange("p i (m t) -> p m i t", t=PACK),
            )
            return grouped

        def quantise(grouped, name, codes=None, scales=None):
            width = grouped.shape[1] // PACK
            if codes is None:
                codes = keep.tile([P, width], U32, name=name + "_codes", align_bytes=64)[:]
            if scales is None:
                scales = keep.tile([P, width], U8, name=name + "_scales", align_bytes=64)[:]
            nc.vector.quantize_mx(out=codes.bitcast(FP8X4), scales=scales, in_=grouped[:])
            return codes, scales

        def codes_in_slot(name, count, tag):
            words = ring.tile([P, count * PASS], U32, name=name, tag=tag, align_bytes=64)
            return [words[:, n * PASS : (n + 1) * PASS] for n in range(count)]

        def planes_in_larger_slot(name, count):
            planes = ring.tile([P, count * PASS], U8, name=name, tag="larger", bufs=LARGER_BUFS, align_bytes=64)
            return [planes[:, n * PASS : (n + 1) * PASS] for n in range(count)]

        v2_scales = pick_halves(tab2_plane[:], idx2, U8, "v2_scales")
        v2_words = pick_halves(tab2_table[:].bitcast(U32), idx2, U32, "v2_words")
        a_mx, w_mx, h_mx = {}, {}, {}
        a_grouped = {(c, 0): round_weight(a_raw[c, 0]) for c in range(2)}
        v_scales = pick_halves(tab_plane[:], idx, U8, "v_scales")
        v_words = [pick_halves(tab_table0[:].bitcast(U32), idx, U32, "v_words0")]
        a0_codes = codes_in_slot("a0_codes", 2, "tab_plane")
        a_mx[0, 0] = quantise(a_grouped[0, 0], "a00", a0_codes[0])

        b4_codes = keep.tile([P, 2 * H], U8, name="b4_codes", align_bytes=64)
        nc.gpsimd.tensor_copy(
            out=b4_codes[:].rearrange("p (b t m e) -> p b t m e", t=PACK, m=P, e=2),
            in_=b4_raw[:].rearrange("p (b m t e) -> p b t m e", t=PACK, m=P, e=2),
        )
        b4_dealt_plane = keep.tile([P, H], U8, name="b4_dealt_plane", align_bytes=64)
        nc.gpsimd.tensor_copy(
            out=b4_dealt_plane[:].rearrange("p (b t m) -> p b t m", t=PACK, m=P),
            in_=b4_plane[:].rearrange("p (b m t) -> p b t m", t=PACK, m=P),
        )
        a_mx[1, 0] = quantise(a_grouped[1, 0], "a10", a0_codes[1])
        v_words.append(
            [pick(tab_table1[:].bitcast(U32), idx, half * HALF, HALF, U32, "v_words1_%d" % half)[:] for half in range(2)]
        )


        q_of = {}

        def contact_projections(units, tag):
            q_rows = ring.tile([P, len(units) * HALF], F32, name="q_rows", tag=tag, align_bytes=64)
            for n, (blk, t, half) in enumerate(units):
                col = blk * PASS + t * P
                q_acc = psum.tile([P, HALF], F32, name="q_acc", tag="q", bufs=Q_BANKS)
                nc.tensor.matmul_mx(
                    q_acc[:],
                    lhsT=b4_codes[:, 2 * col : 2 * (col + P)].bitcast(FP4X4),
                    lhsT_scale=b4_dealt_plane[:, col : col + P],
                    rhs=v2_words[half].bitcast(FP8X4),
                    rhs_scale=v2_scales[half],
                    start=True,
                    stop=True,
                )
                q_of[blk, t, half] = q_rows[:, n * HALF : (n + 1) * HALF]
                nc.scalar.copy(out=q_of[blk, t, half], in_=q_acc[:])

        def larger_projection(blk, t, half, larger):
            cols = slice(t * P, (t + 1) * P)
            p_acc = psum.tile([P, HALF], F32, name="p_acc", tag="p", bufs=P_BANKS)
            for c in range(2):
                codes, scales = a_mx[c, blk]
                nc.tensor.matmul_mx(
                    p_acc[:],
                    lhsT=codes[:, cols].bitcast(FP8X4),
                    lhsT_scale=scales[:, cols],
                    rhs=v_words[c][half].bitcast(FP8X4),
                    rhs_scale=v_scales[half][PACK * c : P, :],
                    start=(c == 0),
                    stop=(c == 1),
                )
            nc.vector.tensor_tensor(larger, p_acc[:], q_of[blk, t, half], ALU.max)

        def new_larger():
            larger = ring.tile([P, HALF], F32, name="larger", tag="larger", bufs=LARGER_BUFS, align_bytes=64)
            return larger[:]

        def new_short(count):
            return ring.tile([P, PACK, count], F32, name="short", tag="short", bufs=SHORT_BUFS)

        def shortfall(row, larger, blk, t, first, count):
            lo = first % HALF
            nc.vector.tensor_tensor(
                row, g_rows[blk, t][:].indirect(offsets(idx, first, count)), larger[:, lo : lo + count], ALU.subtract
            )

        def clamp(short, tag="grouped", bufs=GROUPED_BUFS):
            count = short.shape[2]
            grouped = ring.tile([P, PACK * count], BF16, name="grouped", tag=tag, bufs=bufs, align_bytes=64)
            woven = grouped[:].rearrange("p (c i t) -> p c t i", t=PACK, i=LINE)
            slices = short[:].rearrange("p t (c i) -> p c t i", i=LINE)
            nc.scalar.activation(out=woven, in_=slices, func=ACT.Relu, scale=-1.0)
            return grouped


        out_rows = out.rearrange("(m t) j -> m t j", t=PACK)

        def feature_sums(y_acc, t, first, count):
            lo = first % HALF
            cols = slice(t * P, (t + 1) * P)
            operands = [(h_mx[0, first - lo], slice(lo, lo + count)), (h_mx[1, first], slice(0, count))]
            for blk, ((codes, scales), span) in enumerate(operands):
                nc.tensor.matmul_mx(
                    y_acc,
                    lhsT=w_mx[blk][0][:, cols].bitcast(FP8X4),
                    lhsT_scale=w_mx[blk][1][:, cols],
                    rhs=codes[:, span].bitcast(FP8X4),
                    rhs_scale=scales[:, span],
                    start=(blk == 0),
                    stop=(blk == 1),
                )

        def add_bias(staged, y_acc, t, on_vector=False):
            if on_vector:
                nc.vector.tensor_scalar(staged[:, t, :], y_acc, bias_cols[:, t : t + 1], None, ALU.add)
            else:
                nc.scalar.activation(out=staged[:, t, :], in_=y_acc, func=ACT.Identity, bias=bias_cols[:, t : t + 1])

        def new_staged(count):
            return ring.tile([P, PACK, count], F32, name="staged", tag="raw", bufs=RAW_BUFS, align_bytes=64)


        units = [(0, t, half) for t in range(PACK) for half in range(2)]
        contact_projections(units[:PACK], "a10_raw")
        contact_projections(units[PACK:], "tab_table1")

        short0 = [new_short(HALF) for half in range(2)]
        pending = None
        for blk, t, half in units:
            larger = new_larger()
            larger_projection(blk, t, half, larger)
            if pending:
                shortfall(*pending)
            pending = (short0[half][:, t, :], larger, blk, t, half * HALF, HALF)
            if (t, half) == (1, 0):
                contact_projections([(1, s, 0) for s in range(PACK)], "g00")
                a_grouped[0, 1] = round_weight(a_raw[0, 1])
            if (t, half) == (2, 0):
                a_grouped[1, 1] = round_weight(a_raw[1, 1])
            if (t, half) == (3, 0):
                a1_codes = codes_in_slot("a1_codes", 2, "tab2_table")
                a1_planes = planes_in_larger_slot("a1_scales", 2)
                for c in range(2):
                    a_mx[c, 1] = quantise(a_grouped[c, 1], "a%d1" % c, a1_codes[c], a1_planes[c])
                contact_projections([(1, s, 1) for s in range(PACK)], "g02")
                w0_grouped = round_weight(w_raw[0])
        h0_grouped = [clamp(short0[0])]
        w1_grouped = round_weight(w_raw[1], "g01", 1)
        shortfall(*pending)
        h0_grouped.append(clamp(short0[1]))


        short1 = new_short(HALF)
        pending = None
        for t in range(PACK):
            larger = new_larger()
            larger_projection(1, t, 0, larger)
            if pending:
                shortfall(*pending)
            pending = (short1[:, t, :], larger, 1, t, 0, HALF)
        w0_codes, w1_codes, h00_codes, h01_codes = codes_in_slot("late_codes", 4, "g03")
        w0_plane, h00_plane = planes_in_larger_slot("w0_h00_scales", 2)
        w_mx[0] = quantise(w0_grouped, "w0", w0_codes, w0_plane)
        h_mx[0, 0] = quantise(h0_grouped[0], "h00", h00_codes, h00_plane)
        shortfall(*pending)
        h10_grouped = clamp(short1)
        w1_plane, h01_plane = planes_in_larger_slot("w1_h01_scales", 2)
        h_mx[0, HALF] = quantise(h0_grouped[1], "h01", h01_codes, h01_plane)
        w_mx[1] = quantise(w1_grouped, "w1", w1_codes, w1_plane)


        shorts = [new_short(CHUNK) for n in range(2)]
        kept = ring.tile([P, PACK * HALF], F32, name="kept", tag="g01", bufs=1, align_bytes=64)
        kept_of = [kept[:, t * HALF : (t + 1) * HALF] for t in range(PACK)]
        for t in range(PACK):
            larger_projection(1, t, 1, kept_of[t])
            if t == 1:
                h_mx[1, 0] = quantise(h10_grouped, "h10")
            if t > 0:
                shortfall(shorts[0][:, t - 1, :], kept_of[t - 1], 1, t - 1, *CHUNKS[0])
        shortfall(shorts[0][:, PACK - 1, :], kept_of[PACK - 1], 1, PACK - 1, *CHUNKS[0])

        grouped = clamp(shorts[0], "chunk0", 1)
        last = len(CHUNKS) - 1
        for n in range(1, last):
            if n >= 2:
                shorts.append(ring.tile([P, PACK, CHUNK], F32, name="short", tag="chunk%d" % (n - 2), align_bytes=64))
            for t in range(PACK):
                shortfall(shorts[n][:, t, :], kept_of[t], 1, t, *CHUNKS[n])
            h_mx[1, CHUNKS[n - 1][0]] = quantise(grouped, "h1_%d" % (n - 1))
            grouped = clamp(shorts[n], "chunk%d" % n, 1)

        first = CHUNKS[last][0]
        last_grouped = keep.tile([P, PACK * CHUNK], BF16, name="last_grouped", align_bytes=64)
        last_woven = last_grouped[:].rearrange("p (c t) -> p c t", t=PACK)
        low = ring.tile([P, 2, CHUNK], F32, name="short", tag="chunk%d" % (last - 2), align_bytes=64)
        for t in range(2):
            shortfall(low[:, t, :], kept_of[t], 1, t, first, CHUNK)
        nc.scalar.activation(out=last_woven[:, :, 0:2], in_=low[:].rearrange("p t c -> p c t"), func=ACT.Relu, scale=-1.0)
        h_mx[1, CHUNKS[last - 1][0]] = quantise(grouped, "h1_%d" % (last - 1))
        high = ring.tile([P, 2, CHUNK], F32, name="short", tag="chunk%d" % (last - 1), align_bytes=64)
        for t in range(2, PACK):
            shortfall(high[:, t - 2, :], kept_of[t], 1, t, first, CHUNK)
        nc.vector.tensor_scalar(last_woven[:, :, 2:PACK], high[:].rearrange("p t c -> p c t"), -1.0, 0.0, ALU.mult, ALU.max)
        h_mx[1, first] = quantise(last_grouped, "h1_%d" % last)


        staged = new_staged(HALF)
        for t in range(PACK):
            y_acc = psum.tile([P, HALF], F32, name="y_acc", tag="q", bufs=Q_BANKS)
            feature_sums(y_acc[:], t, 0, HALF)
            add_bias(staged, y_acc[:], t)
            nc.sync.dma_start(out_rows[:, t, 0:HALF], staged[:, t, :])

        for start, count in CHUNKS[:last]:
            staged = new_staged(count)
            y_acc = psum.tile([P, PACK, count], F32, name="y_acc", tag="q", bufs=Q_BANKS)
            for t in range(PACK):
                feature_sums(y_acc[:, t, :], t, start, count)
            for t in range(PACK):
                add_bias(staged, y_acc[:, t, :], t)
            nc.sync.dma_start(out_rows[:, :, start : start + count], staged[:])

        staged = new_staged(CHUNK)
        for t in range(PACK):
            tag, bufs = ("p", P_BANKS) if t < P_BANKS else ("q", Q_BANKS)
            y_acc = psum.tile([P, CHUNK], F32, name="y_acc", tag=tag, bufs=bufs)
            feature_sums(y_acc[:], t, first, CHUNK)
            add_bias(staged, y_acc[:], t, on_vector=t % 2 == 0)
        nc.sync.dma_start(out_rows[:, :, first : first + CHUNK], staged[:])
